import numpy as np
import ml_dtypes


def mxq(x, axis, fmt="e4m3"):
    dtype, down = {"e4m3": (ml_dtypes.float8_e4m3fn, 7), "e5m2": (ml_dtypes.float8_e5m2, 14)}[fmt]
    v = np.moveaxis(np.asarray(x, np.float32).astype(ml_dtypes.bfloat16).astype(np.float64), axis, -1)
    blocks = v.reshape(v.shape[:-1] + (-1, 32))
    amax = np.abs(blocks).max(-1, keepdims=True)
    byte = np.maximum(np.where(amax > 0, np.frexp(amax)[1] - 1 + 127, 0) - down, 1)
    scale = np.exp2(byte - 127.0)
    codes = (blocks / scale).astype(np.float32).astype(dtype).astype(np.float64)
    return np.moveaxis((codes * scale).reshape(v.shape), -1, axis)


WIDE = False


def mx_kscale(k):
    if not WIDE:
        return np.ones(k)
    levels = np.array([30, -30])
    if k % 512:
        return np.exp2(np.random.permutation(np.resize(levels, k // 32))).repeat(32)
    a = np.empty((k // 512, 16))
    for p in range(k // 512):
        a[p, :8] = np.random.permutation(np.resize(levels, 8))
        for g in range(8):
            far = levels[np.abs(levels - a[p, g]) >= 10]
            a[p, g + 8] = far[np.random.randint(len(far))]
    return np.exp2(a.ravel()).repeat(32)


def f64(x):
    return np.asarray(x).astype(np.float64)


def striped(idx):
    return np.tile(np.asarray(idx).reshape(-1, 16).T, (8, 1)).astype(np.uint16)


def unstriped(offs):
    return offs[:16].T.reshape(-1).astype(np.int64)


E2M1 = np.array([0.0, 0.5, 1.0, 1.5, 2.0, 3.0, 4.0, 6.0, -0.0, -0.5, -1.0, -1.5, -2.0, -3.0, -4.0, -6.0])


def pack_weight(w, fmt):
    k, n = w.shape
    w = f64(np.asarray(w, np.float32).astype(ml_dtypes.bfloat16)).reshape(k // 32, 32, n)
    amax = np.abs(w).max(1)
    if fmt == "e4m3":
        byte = np.frexp(amax)[1] - 1 + 127 - 7
    else:
        mant, ex = np.frexp(amax / 6.0)
        byte = np.where(mant > 0.5, ex, ex - 1) + 127
    byte = np.clip(np.where(amax > 0, byte, 1), 1, 254)
    scaled = (w * np.exp2(127.0 - byte)[:, None, :]).reshape(k, n).astype(np.float32)
    by_word = np.ascontiguousarray(scaled.reshape(k // 512, 128, 4, n).transpose(0, 1, 3, 2))
    if fmt == "e4m3":
        words = by_word.astype(ml_dtypes.float8_e4m3fn).view(np.uint8)
    else:
        c = by_word.astype(ml_dtypes.float4_e2m1fn).view(np.uint8) & 0xF
        words = (c[..., 0::2] | (c[..., 1::2] << 4)).reshape(k // 512, 128, 2 * n)
    return np.ascontiguousarray(words), np.ascontiguousarray(byte.astype(np.uint8).reshape(k // 512, 16, n))


def unpack_weight(words, scales, fmt):
    g, _, n = scales.shape
    words = np.ascontiguousarray(words).reshape(g, 128, n, -1)
    if fmt == "e4m3":
        vals = words.view(ml_dtypes.float8_e4m3fn).astype(np.float64)
    else:
        nib = np.empty((g, 128, n, 4), np.uint8)
        nib[..., 0::2] = words & 0xF
        nib[..., 1::2] = words >> 4
        vals = E2M1[nib]
    vals = vals * np.repeat(np.exp2(scales.astype(np.float64) - 127.0), 8, axis=1)[..., None]
    return vals.transpose(0, 1, 3, 2).reshape(g * 512, n)


K, T, J, R, V, N, E = 512, 1024, 256, 512, 512, 256, 1024


def setup_inputs():
    n = np.random.standard_normal
    idx = np.random.permutation(T)[:J]
    idx2 = np.random.permutation(V)[:J]
    idx3 = np.random.permutation(V)[:J]
    idx4 = np.random.permutation(T)[:J]
    idx5 = np.random.permutation(E)[:J]
    fk = mx_kscale(K)
    fr = mx_kscale(R)
    xtp = pack_weight(n((K, T)) / fk[:, None], "e2m1")
    wp = pack_weight(n((K, R)) * 1 / np.sqrt(K) * fk[:, None] * fr, "e4m3")
    wbp = pack_weight(n((R, N)) * 1 / np.sqrt(R) / fr[:, None], "e2m1")
    wsp = pack_weight(n((K, N)) * 1 / np.sqrt(K) * fk[:, None], "e4m3")
    return {
        "xt_words": xtp[0],
        "xt_scales": xtp[1],
        "w_words": wp[0],
        "w_scales": wp[1],
        "tb": (n((R, V)) * 0.8 * fr[:, None]).astype(np.float32),
        "wb_words": wbp[0],
        "wb_scales": wbp[1],
        "ws_words": wsp[0],
        "ws_scales": wsp[1],
        "offs": striped(idx),
        "offs2": striped(idx2),
        "offs3": striped(idx3),
        "offs4": striped(idx4),
        "offs5": striped(idx5),
    }


def reference(xt_words, xt_scales, w_words, w_scales, tb, wb_words, wb_scales, ws_words, ws_scales, offs, offs2, offs3, offs4, offs5):
    idx = unstriped(offs)
    idx2 = unstriped(offs2)
    idx3 = unstriped(offs3)
    idx4 = unstriped(offs4)
    idx5 = unstriped(offs5)
    xtu = unpack_weight(xt_words, xt_scales, "e2m1")
    wu = unpack_weight(w_words, w_scales, "e4m3")
    wbu = unpack_weight(wb_words, wb_scales, "e2m1")
    wsu = unpack_weight(ws_words, ws_scales, "e4m3")
    xtidxg = xtu[:, idx]
    a = wu.T @ xtidxg
    hid = np.maximum(np.minimum(a, f64(tb)[:, idx2]), f64(tb)[:, idx3])
    hidq = mxq(hid, 0, "e5m2")
    xtidx4g = xtu[:, idx4]
    p = wbu.T @ hidq + wsu.T @ xtidx4g
    y = np.zeros((N, E))
    y[:, idx5] = p
    return y

@@ -1,0 +1,169 @@
+from contextlib import ExitStack
+
+import concourse.mybir as mybir
+
+K, T, J, R, V, N, E = 512, 1024, 256, 512, 512, 256, 1024
+FLOPS = 2 * J * (K * R + R * N + K * N)
+
+F32 = mybir.dt.float32
+BF16 = mybir.dt.bfloat16
+I32 = mybir.dt.int32
+U32 = mybir.dt.uint32
+U16 = mybir.dt.uint16
+U8 = mybir.dt.uint8
+E4M3 = mybir.dt.float8_e4m3fn_x4
+E5M2 = mybir.dt.float8_e5m2_x4
+E2M1 = mybir.dt.float4_e2m1fn_x4
+COPY = mybir.ActivationFunctionType.Copy
+MIN = mybir.AluOpType.min
+MAX = mybir.AluOpType.max
+
+P = 128
+PACK = 4
+HALF = J // 2
+LIST_COLS = J // 16
+
+
+def tile_list_clamped_solo_further_scattered_kernel(
+    tc, xt_words, xt_scales, w_words, w_scales, tb, wb_words, wb_scales, ws_words, ws_scales,
+    offs, offs2, offs3, offs4, offs5, out,
+):
+    nc = tc.nc
+    with ExitStack() as ctx:
+        keep = ctx.enter_context(tc.tile_pool(name="keep", bufs=1))
+        psum = ctx.enter_context(tc.psum_pool(name="psum", bufs=1))
+
+        def sb(name, shape, dtype):
+            return keep.tile(shape, dtype, name=name, align_bytes=64)
+
+        def load_list(name, src):
+            tile = keep.tile([P, LIST_COLS], U16, name=name)
+            nc.sync.dma_start(tile[:], src)
+            return tile
+
+        def load_scale_rows(queue, plane, src, q):
+            queue.dma_start(plane[32 * q : 32 * q + 4, :].bitcast(I32), src[0, 4 * q : 4 * q + 4, :].bitcast(I32))
+
+        xt_plane = sb("xt_plane", [P, T], U8)
+        w_plane_in = sb("w_plane_in", [P, R], U8)
+        wb_plane = sb("wb_plane", [P, N], U8)
+        ws_plane = sb("ws_plane", [P, N], U8)
+        for plane in (xt_plane, w_plane_in, wb_plane, ws_plane):
+            nc.vector.memset(plane[:].bitcast(I32), 0)
+        pages = [sb(f"page{b}", [P, E], F32) for b in range(N // P)]
+        for page in pages:
+            nc.vector.memset(page[:], 0.0)
+
+        xt_table = sb("xt_table", [P, T], U16)
+        w_in = sb("w_in", [P, R], U32)
+        tb_rows = tb.rearrange("(p t) v -> p t v", t=PACK)
+        tb0 = sb("tb0", [P, V], F32)
+        tb1 = sb("tb1", [P, V], F32)
+        tb23 = sb("tb23", [P, 2, V], F32)
+        bounds = [tb0[:], tb1[:], tb23[:, 0, :], tb23[:, 1, :]]
+
+        first = load_list("first", offs)
+        upper_list = load_list("upper_list", offs2)
+        lower_list = load_list("lower_list", offs3)
+        nc.scalar.dma_start(xt_table[:].bitcast(I32), xt_words[0].bitcast(I32))
+        nc.scalar.dma_start(tb0[:], tb_rows[:, 0, :])
+        nc.scalar.dma_start(w_in[:].bitcast(I32), w_words[0].rearrange("p c r -> p (c r)").bitcast(I32))
+        nc.scalar.dma_start(tb1[:], tb_rows[:, 1, :])
+        nc.scalar.dma_start(tb23[:], tb_rows[:, 2:4, :])
+        for q in range(4):
+            load_scale_rows(nc.sync, xt_plane, xt_scales, q)
+        load_scale_rows(nc.sync, w_plane_in, w_scales, 0)
+        for q in range(1, 4):
+            load_scale_rows(nc.gpsimd, w_plane_in, w_scales, q)
+        further = load_list("further", offs4)
+        places = load_list("places", offs5)
+        ws_codes = sb("ws_codes", [P, N], U32)
+        wb_codes = sb("wb_codes", [P, N], U16)
+        nc.sync.dma_start(ws_codes[:].bitcast(I32), ws_words[0].rearrange("p c r -> p (c r)").bitcast(I32))
+        for q in range(4):
+            load_scale_rows(nc.sync, ws_plane, ws_scales, q)
+        nc.sync.dma_start(wb_codes[:].bitcast(I32), wb_words[0].bitcast(I32))
+        for q in range(4):
+            load_scale_rows(nc.gpsimd, wb_plane, wb_scales, q)
+
+        x1_codes = sb("x1_codes", [P, J], U16)
+        x1_plane = sb("x1_plane", [P, J], U8)
+        x4_codes = sb("x4_codes", [P, J], U16)
+        x4_plane = sb("x4_plane", [P, J], U8)
+        w_codes = sb("w_codes", [P, PACK, P], U32)
+        w_plane = sb("w_plane", [P, PACK, P], U8)
+        upper = sb("upper", [P, PACK, J], F32)
+        lower = sb("lower", [P, PACK, J], F32)
+
+        nc.vector.tensor_copy(x1_codes[:], xt_table[:].indirect(first[:]))
+        nc.vector.tensor_copy(lower[:, 0, :], bounds[0].indirect(lower_list[:]))
+        nc.vector.tensor_copy(w_codes[:], w_in[:].rearrange("p (m t) -> p t m", t=PACK))
+        nc.vector.tensor_copy(x1_plane[:], xt_plane[:].indirect(first[:]))
+        nc.vector.tensor_copy(w_plane[:], w_plane_in[:].rearrange("p (m t) -> p t m", t=PACK))
+        nc.vector.tensor_copy(x4_codes[:], xt_table[:].indirect(further[:]))
+        nc.vector.tensor_copy(x4_plane[:], xt_plane[:].indirect(further[:]))
+
+        nc.scalar.activation(upper[:, 0, :], bounds[0].indirect(upper_list[:]), COPY)
+        nc.scalar.activation(upper[:, 1, :], bounds[1].indirect(upper_list[:]), COPY)
+        nc.scalar.activation(lower[:, 1, :], bounds[1].indirect(lower_list[:]), COPY)
+        nc.scalar.activation(upper[:, 2, :], bounds[2].indirect(upper_list[:]), COPY)
+        nc.scalar.activation(upper[:, 3, :], bounds[3].indirect(upper_list[:]), COPY)
+        halves = [slice(h * HALF, (h + 1) * HALF) for h in range(2)]
+        list_halves = [slice(h * LIST_COLS // 2, (h + 1) * LIST_COLS // 2) for h in range(2)]
+        for h in range(2):
+            for t in (2, 3):
+                nc.scalar.activation(lower[:, t, halves[h]], bounds[t].indirect(lower_list[:, list_halves[h]]), COPY)
+
+        a_banks = [psum.tile([P, PACK, HALF], F32, name=f"a{h}") for h in range(2)]
+        for h in range(2):
+            for t in range(PACK):
+                nc.tensor.matmul_mx(
+                    out=a_banks[h][:, t, :],
+                    lhsT=w_codes[:, t, :].bitcast(E4M3), lhsT_scale=w_plane[:, t, :],
+                    rhs=x1_codes[:, halves[h]].bitcast(E2M1), rhs_scale=x1_plane[:, halves[h]],
+                    start=True, stop=True,
+                )
+        p_banks = [[psum.tile([P, HALF], F32, name=f"p{h}{b}") for b in range(2)] for h in range(2)]
+        for h in range(2):
+            for b in range(2):
+                cols = slice(b * P, (b + 1) * P)
+                nc.tensor.matmul_mx(
+                    out=p_banks[h][b][:],
+                    lhsT=ws_codes[:, cols].bitcast(E4M3), lhsT_scale=ws_plane[:, cols],
+                    rhs=x4_codes[:, halves[h]].bitcast(E2M1), rhs_scale=x4_plane[:, halves[h]],
+                    start=True, stop=False,
+                )
+
+        capped = [sb(f"capped{h}", [P, PACK, HALF], F32) for h in range(2)]
+        for h in range(2):
+            nc.vector.tensor_tensor(capped[h][:], a_banks[h][:], upper[:, :, halves[h]], MIN)
+        for h in range(2):
+            hid = sb(f"hid{h}", [P, HALF * PACK], BF16)
+            nc.vector.tensor_tensor(
+                hid[:].rearrange("p (c i t) -> p c t i", i=4, t=PACK),
+                capped[h][:].rearrange("p t (c i) -> p c t i", i=4),
+                lower[:, :, halves[h]].rearrange("p t (c i) -> p c t i", i=4),
+                MAX,
+            )
+            hid_codes = sb(f"hid_codes{h}", [P, HALF], U32)
+            hid_plane = sb(f"hid_plane{h}", [P, HALF], U8)
+            nc.vector.quantize_mx(out=hid_codes[:].bitcast(E5M2), scales=hid_plane[:], in_=hid[:])
+            for b in range(2):
+                cols = slice(b * P, (b + 1) * P)
+                nc.tensor.matmul_mx(
+                    out=p_banks[h][b][:],
+                    lhsT=wb_codes[:, cols].bitcast(E2M1), lhsT_scale=wb_plane[:, cols],
+                    rhs=hid_codes[:].bitcast(E5M2), rhs_scale=hid_plane[:],
+                    start=False, stop=True,
+                )
+
+        for h in range(2):
+            slots = places[:, list_halves[h]]
+            sums1 = sb(f"sums{h}1", [P, HALF], F32)
+            nc.scalar.copy(sums1[:], p_banks[h][1][:])
+            sums0 = sb(f"sums{h}0", [P, HALF], F32)
+            nc.scalar.copy(sums0[:], p_banks[h][0][:])
+            nc.scalar.activation(pages[1][:].indirect(slots), sums1[:], COPY)
+            nc.vector.tensor_copy(pages[0][:].indirect(slots), sums0[:])
+        nc.sync.dma_start(out[0:P, :], pages[0][:])
+        nc.scalar.dma_start(out[P : 2 * P, :], pages[1][:])

@@ -20,8 +20,10 @@ MAX = mybir.AluOpType.max
 
 P = 128
 PACK = 4
+QUADRANTS = 4
 HALF = J // 2
 LIST_COLS = J // 16
+RUN = 4
 
 
 def tile_list_clamped_solo_further_scattered_kernel(
@@ -50,66 +52,75 @@ def tile_list_clamped_solo_further_scattered_kernel(
         ws_plane = sb("ws_plane", [P, N], U8)
         for plane in (xt_plane, w_plane_in, wb_plane, ws_plane):
             nc.vector.memset(plane[:].bitcast(I32), 0)
+        warm_in = sb("warm_in", [P, 1], F32)
+        warm_out = sb("warm_out", [P, 1], F32)
+        nc.vector.memset(warm_in[:], 0.0)
         pages = [sb(f"page{b}", [P, E], F32) for b in range(N // P)]
         for page in pages:
-            nc.vector.memset(page[:], 0.0)
+            nc.vector.memset(page[:, 0 : E - 1], 0.0)
+            nc.vector.memset(page[:, E - 1 : E], 0.0)
 
         xt_table = sb("xt_table", [P, T], U16)
         w_in = sb("w_in", [P, R], U32)
+        ws_codes = sb("ws_codes", [P, N], U32)
+        wb_codes = sb("wb_codes", [P, N], U16)
         tb_rows = tb.rearrange("(p t) v -> p t v", t=PACK)
         tb0 = sb("tb0", [P, V], F32)
         tb1 = sb("tb1", [P, V], F32)
         tb23 = sb("tb23", [P, 2, V], F32)
         bounds = [tb0[:], tb1[:], tb23[:, 0, :], tb23[:, 1, :]]
 
-        first = load_list("first", offs)
         upper_list = load_list("upper_list", offs2)
+        nc.scalar.dma_start(tb0[:], tb_rows[:, 0, :])
         lower_list = load_list("lower_list", offs3)
         nc.scalar.dma_start(xt_table[:].bitcast(I32), xt_words[0].bitcast(I32))
-        nc.scalar.dma_start(tb0[:], tb_rows[:, 0, :])
-        nc.scalar.dma_start(w_in[:].bitcast(I32), w_words[0].rearrange("p c r -> p (c r)").bitcast(I32))
+        first_list = load_list("first_list", offs)
         nc.scalar.dma_start(tb1[:], tb_rows[:, 1, :])
+        further_list = load_list("further_list", offs4)
+        nc.scalar.dma_start(w_in[:].bitcast(I32), w_words[0].rearrange("p c r -> p (c r)").bitcast(I32))
+        nc.scalar.activation(warm_out[:], warm_in[:], COPY)
         nc.scalar.dma_start(tb23[:], tb_rows[:, 2:4, :])
-        for q in range(4):
+        load_scale_rows(nc.gpsimd, xt_plane, xt_scales, QUADRANTS - 1)
+        load_scale_rows(nc.gpsimd, w_plane_in, w_scales, QUADRANTS - 1)
+        load_scale_rows(nc.gpsimd, wb_plane, wb_scales, 0)
+        for q in range(QUADRANTS - 1):
             load_scale_rows(nc.sync, xt_plane, xt_scales, q)
-        load_scale_rows(nc.sync, w_plane_in, w_scales, 0)
-        for q in range(1, 4):
-            load_scale_rows(nc.gpsimd, w_plane_in, w_scales, q)
-        further = load_list("further", offs4)
-        places = load_list("places", offs5)
-        ws_codes = sb("ws_codes", [P, N], U32)
-        wb_codes = sb("wb_codes", [P, N], U16)
+        for q in range(QUADRANTS - 1):
+            load_scale_rows(nc.sync, w_plane_in, w_scales, q)
         nc.sync.dma_start(ws_codes[:].bitcast(I32), ws_words[0].rearrange("p c r -> p (c r)").bitcast(I32))
-        for q in range(4):
-            load_scale_rows(nc.sync, ws_plane, ws_scales, q)
         nc.sync.dma_start(wb_codes[:].bitcast(I32), wb_words[0].bitcast(I32))
-        for q in range(4):
-            load_scale_rows(nc.gpsimd, wb_plane, wb_scales, q)
+        for q in range(QUADRANTS):
+            load_scale_rows(nc.sync, ws_plane, ws_scales, q)
+        for q in range(1, QUADRANTS):
+            load_scale_rows(nc.sync, wb_plane, wb_scales, q)
+        place_list = load_list("place_list", offs5)
 
-        x1_codes = sb("x1_codes", [P, J], U16)
-        x1_plane = sb("x1_plane", [P, J], U8)
-        x4_codes = sb("x4_codes", [P, J], U16)
-        x4_plane = sb("x4_plane", [P, J], U8)
+        first_codes = sb("first_codes", [P, J], U16)
+        first_plane = sb("first_plane", [P, J], U8)
+        further_codes = sb("further_codes", [P, J], U16)
+        further_plane = sb("further_plane", [P, J], U8)
         w_codes = sb("w_codes", [P, PACK, P], U32)
         w_plane = sb("w_plane", [P, PACK, P], U8)
         upper = sb("upper", [P, PACK, J], F32)
         lower = sb("lower", [P, PACK, J], F32)
-
-        nc.vector.tensor_copy(x1_codes[:], xt_table[:].indirect(first[:]))
-        nc.vector.tensor_copy(lower[:, 0, :], bounds[0].indirect(lower_list[:]))
-        nc.vector.tensor_copy(w_codes[:], w_in[:].rearrange("p (m t) -> p t m", t=PACK))
-        nc.vector.tensor_copy(x1_plane[:], xt_plane[:].indirect(first[:]))
-        nc.vector.tensor_copy(w_plane[:], w_plane_in[:].rearrange("p (m t) -> p t m", t=PACK))
-        nc.vector.tensor_copy(x4_codes[:], xt_table[:].indirect(further[:]))
-        nc.vector.tensor_copy(x4_plane[:], xt_plane[:].indirect(further[:]))
-
-        nc.scalar.activation(upper[:, 0, :], bounds[0].indirect(upper_list[:]), COPY)
-        nc.scalar.activation(upper[:, 1, :], bounds[1].indirect(upper_list[:]), COPY)
-        nc.scalar.activation(lower[:, 1, :], bounds[1].indirect(lower_list[:]), COPY)
-        nc.scalar.activation(upper[:, 2, :], bounds[2].indirect(upper_list[:]), COPY)
-        nc.scalar.activation(upper[:, 3, :], bounds[3].indirect(upper_list[:]), COPY)
         halves = [slice(h * HALF, (h + 1) * HALF) for h in range(2)]
         list_halves = [slice(h * LIST_COLS // 2, (h + 1) * LIST_COLS // 2) for h in range(2)]
+
+        nc.vector.tensor_copy(first_codes[:], xt_table[:].indirect(first_list[:]))
+        nc.vector.tensor_copy(further_codes[:], xt_table[:].indirect(further_list[:]))
+        nc.vector.tensor_copy(
+            w_codes[:].rearrange("p t (c i) -> p c t i", i=RUN),
+            w_in[:].rearrange("p (c i t) -> p c t i", i=RUN, t=PACK),
+        )
+        nc.vector.tensor_copy(first_plane[:], xt_plane[:].indirect(first_list[:]))
+        nc.vector.tensor_copy(further_plane[:], xt_plane[:].indirect(further_list[:]))
+        nc.vector.tensor_copy(w_plane[:], w_plane_in[:].rearrange("p (m t) -> p t m", t=PACK))
+
+        for t in (0, 1):
+            nc.scalar.activation(upper[:, t, :], bounds[t].indirect(upper_list[:]), COPY)
+            nc.scalar.activation(lower[:, t, :], bounds[t].indirect(lower_list[:]), COPY)
+        for t in (2, 3):
+            nc.scalar.activation(upper[:, t, :], bounds[t].indirect(upper_list[:]), COPY)
         for h in range(2):
             for t in (2, 3):
                 nc.scalar.activation(lower[:, t, halves[h]], bounds[t].indirect(lower_list[:, list_halves[h]]), COPY)
@@ -120,7 +131,7 @@ def tile_list_clamped_solo_further_scattered_kernel(
                 nc.tensor.matmul_mx(
                     out=a_banks[h][:, t, :],
                     lhsT=w_codes[:, t, :].bitcast(E4M3), lhsT_scale=w_plane[:, t, :],
-                    rhs=x1_codes[:, halves[h]].bitcast(E2M1), rhs_scale=x1_plane[:, halves[h]],
+                    rhs=first_codes[:, halves[h]].bitcast(E2M1), rhs_scale=first_plane[:, halves[h]],
                     start=True, stop=True,
                 )
         p_banks = [[psum.tile([P, HALF], F32, name=f"p{h}{b}") for b in range(2)] for h in range(2)]
@@ -130,7 +141,7 @@ def tile_list_clamped_solo_further_scattered_kernel(
                 nc.tensor.matmul_mx(
                     out=p_banks[h][b][:],
                     lhsT=ws_codes[:, cols].bitcast(E4M3), lhsT_scale=ws_plane[:, cols],
-                    rhs=x4_codes[:, halves[h]].bitcast(E2M1), rhs_scale=x4_plane[:, halves[h]],
+                    rhs=further_codes[:, halves[h]].bitcast(E2M1), rhs_scale=further_plane[:, halves[h]],
                     start=True, stop=False,
                 )
 
@@ -140,9 +151,9 @@ def tile_list_clamped_solo_further_scattered_kernel(
         for h in range(2):
             hid = sb(f"hid{h}", [P, HALF * PACK], BF16)
             nc.vector.tensor_tensor(
-                hid[:].rearrange("p (c i t) -> p c t i", i=4, t=PACK),
-                capped[h][:].rearrange("p t (c i) -> p c t i", i=4),
-                lower[:, :, halves[h]].rearrange("p t (c i) -> p c t i", i=4),
+                hid[:].rearrange("p (c i t) -> p c t i", i=RUN, t=PACK),
+                capped[h][:].rearrange("p t (c i) -> p c t i", i=RUN),
+                lower[:, :, halves[h]].rearrange("p t (c i) -> p c t i", i=RUN),
                 MAX,
             )
             hid_codes = sb(f"hid_codes{h}", [P, HALF], U32)
@@ -157,13 +168,11 @@ def tile_list_clamped_solo_further_scattered_kernel(
                     start=False, stop=True,
                 )
 
+        sums = [sb(f"sums{b}", [P, J], F32) for b in range(2)]
         for h in range(2):
-            slots = places[:, list_halves[h]]
-            sums1 = sb(f"sums{h}1", [P, HALF], F32)
-            nc.scalar.copy(sums1[:], p_banks[h][1][:])
-            sums0 = sb(f"sums{h}0", [P, HALF], F32)
-            nc.scalar.copy(sums0[:], p_banks[h][0][:])
-            nc.scalar.activation(pages[1][:].indirect(slots), sums1[:], COPY)
-            nc.vector.tensor_copy(pages[0][:].indirect(slots), sums0[:])
+            nc.vector.tensor_copy(sums[0][:, halves[h]], p_banks[h][0][:])
+            nc.scalar.copy(sums[1][:, halves[h]], p_banks[h][1][:])
+        nc.vector.tensor_copy(pages[0][:].indirect(place_list[:]), sums[0][:])
+        nc.scalar.activation(pages[1][:].indirect(place_list[:]), sums[1][:], COPY)
         nc.sync.dma_start(out[0:P, :], pages[0][:])
         nc.scalar.dma_start(out[P : 2 * P, :], pages[1][:])

from contextlib import ExitStack

import concourse.mybir as mybir

K, T, J, R, V, N, E = 512, 1024, 256, 512, 512, 256, 1024
FLOPS = 2 * J * (K * R + R * N + K * N)

F32 = mybir.dt.float32
BF16 = mybir.dt.bfloat16
I32 = mybir.dt.int32
U32 = mybir.dt.uint32
U16 = mybir.dt.uint16
U8 = mybir.dt.uint8
E4M3 = mybir.dt.float8_e4m3fn_x4
E5M2 = mybir.dt.float8_e5m2_x4
E2M1 = mybir.dt.float4_e2m1fn_x4
COPY = mybir.ActivationFunctionType.Copy
MIN = mybir.AluOpType.min
MAX = mybir.AluOpType.max

P = 128
PACK = 4
QUADRANTS = 4
HALF = J // 2
LIST_COLS = J // 16
RUN = 4


def tile_list_clamped_solo_further_scattered_kernel(
    tc, xt_words, xt_scales, w_words, w_scales, tb, wb_words, wb_scales, ws_words, ws_scales,
    offs, offs2, offs3, offs4, offs5, out,
):
    nc = tc.nc
    with ExitStack() as ctx:
        keep = ctx.enter_context(tc.tile_pool(name="keep", bufs=1))
        psum = ctx.enter_context(tc.psum_pool(name="psum", bufs=1))

        def sb(name, shape, dtype):
            return keep.tile(shape, dtype, name=name, align_bytes=64)

        def load_list(name, src):
            tile = keep.tile([P, LIST_COLS], U16, name=name)
            nc.sync.dma_start(tile[:], src)
            return tile

        def load_scale_rows(queue, plane, src, q):
            queue.dma_start(plane[32 * q : 32 * q + 4, :].bitcast(I32), src[0, 4 * q : 4 * q + 4, :].bitcast(I32))

        xt_plane = sb("xt_plane", [P, T], U8)
        w_plane_in = sb("w_plane_in", [P, R], U8)
        wb_plane = sb("wb_plane", [P, N], U8)
        ws_plane = sb("ws_plane", [P, N], U8)
        for plane in (xt_plane, w_plane_in, wb_plane, ws_plane):
            nc.vector.memset(plane[:].bitcast(I32), 0)
        warm_in = sb("warm_in", [P, 1], F32)
        warm_out = sb("warm_out", [P, 1], F32)
        nc.vector.memset(warm_in[:], 0.0)
        pages = [sb(f"page{b}", [P, E], F32) for b in range(N // P)]
        for page in pages:
            nc.vector.memset(page[:, 0 : E - 1], 0.0)
            nc.vector.memset(page[:, E - 1 : E], 0.0)

        xt_table = sb("xt_table", [P, T], U16)
        w_in = sb("w_in", [P, R], U32)
        ws_codes = sb("ws_codes", [P, N], U32)
        wb_codes = sb("wb_codes", [P, N], U16)
        tb_rows = tb.rearrange("(p t) v -> p t v", t=PACK)
        tb0 = sb("tb0", [P, V], F32)
        tb1 = sb("tb1", [P, V], F32)
        tb23 = sb("tb23", [P, 2, V], F32)
        bounds = [tb0[:], tb1[:], tb23[:, 0, :], tb23[:, 1, :]]

        upper_list = load_list("upper_list", offs2)
        nc.scalar.dma_start(tb0[:], tb_rows[:, 0, :])
        lower_list = load_list("lower_list", offs3)
        nc.scalar.dma_start(xt_table[:].bitcast(I32), xt_words[0].bitcast(I32))
        first_list = load_list("first_list", offs)
        nc.scalar.dma_start(tb1[:], tb_rows[:, 1, :])
        further_list = load_list("further_list", offs4)
        nc.scalar.dma_start(w_in[:].bitcast(I32), w_words[0].rearrange("p c r -> p (c r)").bitcast(I32))
        nc.scalar.activation(warm_out[:], warm_in[:], COPY)
        nc.scalar.dma_start(tb23[:], tb_rows[:, 2:4, :])
        load_scale_rows(nc.gpsimd, xt_plane, xt_scales, QUADRANTS - 1)
        load_scale_rows(nc.gpsimd, w_plane_in, w_scales, QUADRANTS - 1)
        load_scale_rows(nc.gpsimd, wb_plane, wb_scales, 0)
        for q in range(QUADRANTS - 1):
            load_scale_rows(nc.sync, xt_plane, xt_scales, q)
        for q in range(QUADRANTS - 1):
            load_scale_rows(nc.sync, w_plane_in, w_scales, q)
        nc.sync.dma_start(ws_codes[:].bitcast(I32), ws_words[0].rearrange("p c r -> p (c r)").bitcast(I32))
        nc.sync.dma_start(wb_codes[:].bitcast(I32), wb_words[0].bitcast(I32))
        for q in range(QUADRANTS):
            load_scale_rows(nc.sync, ws_plane, ws_scales, q)
        for q in range(1, QUADRANTS):
            load_scale_rows(nc.sync, wb_plane, wb_scales, q)
        place_list = load_list("place_list", offs5)

        first_codes = sb("first_codes", [P, J], U16)
        first_plane = sb("first_plane", [P, J], U8)
        further_codes = sb("further_codes", [P, J], U16)
        further_plane = sb("further_plane", [P, J], U8)
        w_codes = sb("w_codes", [P, PACK, P], U32)
        w_plane = sb("w_plane", [P, PACK, P], U8)
        upper = sb("upper", [P, PACK, J], F32)
        lower = sb("lower", [P, PACK, J], F32)
        halves = [slice(h * HALF, (h + 1) * HALF) for h in range(2)]
        list_halves = [slice(h * LIST_COLS // 2, (h + 1) * LIST_COLS // 2) for h in range(2)]

        nc.vector.tensor_copy(first_codes[:], xt_table[:].indirect(first_list[:]))
        nc.vector.tensor_copy(further_codes[:], xt_table[:].indirect(further_list[:]))
        nc.vector.tensor_copy(
            w_codes[:].rearrange("p t (c i) -> p c t i", i=RUN),
            w_in[:].rearrange("p (c i t) -> p c t i", i=RUN, t=PACK),
        )
        nc.vector.tensor_copy(first_plane[:], xt_plane[:].indirect(first_list[:]))
        nc.vector.tensor_copy(further_plane[:], xt_plane[:].indirect(further_list[:]))
        nc.vector.tensor_copy(w_plane[:], w_plane_in[:].rearrange("p (m t) -> p t m", t=PACK))

        for t in (0, 1):
            nc.scalar.activation(upper[:, t, :], bounds[t].indirect(upper_list[:]), COPY)
            nc.scalar.activation(lower[:, t, :], bounds[t].indirect(lower_list[:]), COPY)
        for t in (2, 3):
            nc.scalar.activation(upper[:, t, :], bounds[t].indirect(upper_list[:]), COPY)
        for h in range(2):
            for t in (2, 3):
                nc.scalar.activation(lower[:, t, halves[h]], bounds[t].indirect(lower_list[:, list_halves[h]]), COPY)

        a_banks = [psum.tile([P, PACK, HALF], F32, name=f"a{h}") for h in range(2)]
        for h in range(2):
            for t in range(PACK):
                nc.tensor.matmul_mx(
                    out=a_banks[h][:, t, :],
                    lhsT=w_codes[:, t, :].bitcast(E4M3), lhsT_scale=w_plane[:, t, :],
                    rhs=first_codes[:, halves[h]].bitcast(E2M1), rhs_scale=first_plane[:, halves[h]],
                    start=True, stop=True,
                )
        p_banks = [[psum.tile([P, HALF], F32, name=f"p{h}{b}") for b in range(2)] for h in range(2)]
        for h in range(2):
            for b in range(2):
                cols = slice(b * P, (b + 1) * P)
                nc.tensor.matmul_mx(
                    out=p_banks[h][b][:],
                    lhsT=ws_codes[:, cols].bitcast(E4M3), lhsT_scale=ws_plane[:, cols],
                    rhs=further_codes[:, halves[h]].bitcast(E2M1), rhs_scale=further_plane[:, halves[h]],
                    start=True, stop=False,
                )

        capped = [sb(f"capped{h}", [P, PACK, HALF], F32) for h in range(2)]
        for h in range(2):
            nc.vector.tensor_tensor(capped[h][:], a_banks[h][:], upper[:, :, halves[h]], MIN)
        for h in range(2):
            hid = sb(f"hid{h}", [P, HALF * PACK], BF16)
            nc.vector.tensor_tensor(
                hid[:].rearrange("p (c i t) -> p c t i", i=RUN, t=PACK),
                capped[h][:].rearrange("p t (c i) -> p c t i", i=RUN),
                lower[:, :, halves[h]].rearrange("p t (c i) -> p c t i", i=RUN),
                MAX,
            )
            hid_codes = sb(f"hid_codes{h}", [P, HALF], U32)
            hid_plane = sb(f"hid_plane{h}", [P, HALF], U8)
            nc.vector.quantize_mx(out=hid_codes[:].bitcast(E5M2), scales=hid_plane[:], in_=hid[:])
            for b in range(2):
                cols = slice(b * P, (b + 1) * P)
                nc.tensor.matmul_mx(
                    out=p_banks[h][b][:],
                    lhsT=wb_codes[:, cols].bitcast(E2M1), lhsT_scale=wb_plane[:, cols],
                    rhs=hid_codes[:].bitcast(E5M2), rhs_scale=hid_plane[:],
                    start=False, stop=True,
                )

        sums = [sb(f"sums{b}", [P, J], F32) for b in range(2)]
        for h in range(2):
            nc.vector.tensor_copy(sums[0][:, halves[h]], p_banks[h][0][:])
            nc.scalar.copy(sums[1][:, halves[h]], p_banks[h][1][:])
        nc.vector.tensor_copy(pages[0][:].indirect(place_list[:]), sums[0][:])
        nc.scalar.activation(pages[1][:].indirect(place_list[:]), sums[1][:], COPY)
        nc.sync.dma_start(out[0:P, :], pages[0][:])
        nc.scalar.dma_start(out[P : 2 * P, :], pages[1][:])
